import numpy as np
import ml_dtypes


def mxq(x, axis, fmt="e4m3"):
    dtype, down = {"e4m3": (ml_dtypes.float8_e4m3fn, 7), "e5m2": (ml_dtypes.float8_e5m2, 14)}[fmt]
    v = np.moveaxis(np.asarray(x, np.float32).astype(ml_dtypes.bfloat16).astype(np.float64), axis, -1)
    blocks = v.reshape(v.shape[:-1] + (-1, 32))
    amax = np.abs(blocks).max(-1, keepdims=True)
    byte = np.maximum(np.where(amax > 0, np.frexp(amax)[1] - 1 + 127, 0) - down, 1)
    scale = np.exp2(byte - 127.0)
    codes = (blocks / scale).astype(np.float32).astype(dtype).astype(np.float64)
    return np.moveaxis((codes * scale).reshape(v.shape), -1, axis)


WIDE = False


def mx_kscale(k, group=512):
    if not WIDE:
        return np.ones(k)
    levels = np.array([10, -10, 5, -5, 0])
    if group != 512:
        return np.exp2(np.random.permutation(np.resize(levels, k // group))).repeat(group)
    if k % 512:
        return np.exp2(np.random.permutation(np.resize(levels, k // 32))).repeat(32)
    a = np.empty((k // 512, 16))
    for p in range(k // 512):
        a[p, :8] = np.random.permutation(np.resize(levels, 8))
        for g in range(8):
            far = levels[np.abs(levels - a[p, g]) >= 10]
            a[p, g + 8] = far[np.random.randint(len(far))]
    return np.exp2(a.ravel()).repeat(32)


def f64(x):
    return np.asarray(x).astype(np.float64)


def striped(idx):
    return np.tile(np.asarray(idx).reshape(-1, 16).T, (8, 1)).astype(np.uint16)


def unstriped(offs):
    return offs[:16].T.reshape(-1).astype(np.int64)


H, KV, D, NQ, N = 4, 4, 256, 512, 512


def setup_inputs():
    n = np.random.standard_normal
    s = mx_kscale(D, 0)[:, None]
    u = mx_kscale(N)
    t = np.random.uniform(0.5, 2.0, N) * u
    v = n((KV, N, 128))
    return {
        "qT": (n((H, D, NQ)) * s * (0.70 / np.sqrt(D))).astype(np.float32),
        "kT": (n((KV, D, N)) / s).astype(np.float32),
        "t": t.reshape(N, 1).astype(np.float32),
        "v": (v / t[:, None]).astype(np.float32),
        "mask": (np.arange(N)[:, None] <= np.sort(np.random.randint(N // 4, N, NQ))[None, :]).astype(np.float32),
    }


def reference(qT, kT, t, v, mask):
    a = mxq(f64(kT), 1, "e4m3").transpose(0, 2, 1) @ mxq(f64(qT), 1, "e4m3")
    p = a / (1.0 + np.exp(-a))
    p = p * f64(mask)
    w = p * f64(t)
    y = mxq(w, 1, "e4m3").transpose(0, 2, 1) @ mxq(f64(v), 1, "e4m3")
    y = y / 16.0
    return y

@@ -1,0 +1,234 @@
+from contextlib import ExitStack
+
+import concourse.mybir as mybir
+
+H, D, NQ, N, E = 4, 256, 512, 512, 128
+FLOPS = 2 * H * D * N * NQ + 2 * H * N * NQ * E
+
+F32 = mybir.dt.float32
+BF16 = mybir.dt.bfloat16
+U32 = mybir.dt.uint32
+U8 = mybir.dt.uint8
+FP8X4 = mybir.dt.float8_e4m3fn_x4
+ACT = mybir.ActivationFunctionType
+ALU = mybir.AluOpType
+
+P = 128
+PACK = 4
+ROWS = 64
+CHUNK = 128
+HALF = 256
+
+
+def tile_rows_a_silu_mask_kernel(tc, qT, kT, t, v, mask, out):
+    nc = tc.nc
+    with ExitStack() as ctx:
+        sb = ctx.enter_context(tc.tile_pool(name="sb", bufs=1))
+        ps = ctx.enter_context(tc.psum_pool(name="ps", bufs=1))
+        ctx.enter_context(tc.manual_schedule())
+
+        def tile(shape, dtype, name):
+            return sb.tile(shape, dtype, name=name, align_bytes=64)
+
+        def copy(engine, dst, src):
+            if engine == "v":
+                nc.vector.tensor_copy(out=dst, in_=src)
+            else:
+                nc.scalar.copy(out=dst, in_=src)
+
+        k_raw, q_raw, m_raw = {}, {}, {}
+
+        def load_k(pair):
+            k_raw[pair] = tile([P, PACK, N], F32, "k_raw%d" % pair)
+            nc.sync.dma_start(out=k_raw[pair][:], in_=kT[2 * pair : 2 * pair + 2].rearrange("g (p j) n -> (g p) j n", j=PACK))
+
+        def load_q(pair, first, count):
+            raw = tile([P, PACK, count * HALF], F32, "q_raw%d_%d" % (pair, first))
+            src = qT[2 * pair : 2 * pair + 2].rearrange("g (p j) n -> (g p) j n", j=PACK)
+            nc.sync.dma_start(out=raw[:], in_=src[:, :, first * HALF : (first + count) * HALF])
+            for i in range(count):
+                q_raw[pair, first + i] = raw[:, :, i * HALF : (i + 1) * HALF]
+
+        def load_mask(half):
+            m_raw[half] = tile([P, PACK, HALF], F32, "m_raw%d" % half)
+            src = mask.rearrange("(p r) q -> p r q", r=PACK)
+            nc.sync.dma_start(out=m_raw[half][:], in_=src[:, :, half * HALF : (half + 1) * HALF])
+
+        t_sb = tile([P, PACK], F32, "t_sb")
+        v_raw = tile([P, H, PACK, E], F32, "v_raw")
+        load_k(0)
+        nc.scalar.dma_start(out=t_sb[:], in_=t.rearrange("(p r) o -> p (r o)", r=PACK))
+        load_q(0, 0, 1)
+        load_mask(0)
+        load_q(0, 1, 1)
+        load_mask(1)
+        load_k(1)
+        load_q(1, 0, 2)
+        nc.sync.dma_start(out=v_raw[:], in_=v.rearrange("h (p j) e -> p h j e", j=PACK))
+
+        staged, codes, scales = {}, {}, {}
+
+        def round_k(engine, pair, half):
+            dst = tile([P, 2, CHUNK, PACK], BF16, "k_bf%d_%d" % (pair, half))
+            src = k_raw[pair][:].rearrange("p j (s r) -> p s j r", r=PACK)[:, :, :, 2 * half : 2 * half + 2]
+            copy(engine, dst[:].rearrange("p r s j -> p s j r"), src)
+            staged["k", pair, half] = dst[:].rearrange("p r s j -> p (r s j)")
+
+        def round_q(engine, pair, half):
+            dst = tile([P, HALF, PACK], BF16, "q_bf%d_%d" % (pair, half))
+            src = q_raw[pair, half].rearrange("p j (c i) -> p c j i", i=4)
+            copy(engine, dst[:].rearrange("p (c i) j -> p c j i", i=4), src)
+            staged["q", pair, half] = dst[:].rearrange("p q j -> p (q j)")
+
+        def round_v(engine, pair):
+            dst = tile([P, 2, E, PACK], BF16, "v_bf%d" % pair)
+            src = v_raw[:, 2 * pair : 2 * pair + 2].rearrange("p g j (c i) -> p g c j i", i=4)
+            copy(engine, dst[:].rearrange("p g (c i) j -> p g c j i", i=4), src)
+            staged["v", pair, 0] = dst[:].rearrange("p g e j -> p (g e j)")
+
+        def quantise(*key):
+            name = "%s%d_%d" % key
+            codes[key] = tile([P, 256], U32, "codes_" + name)
+            scales[key] = tile([P, 256], U8, "scales_" + name)
+            nc.vector.quantize_mx(out=codes[key][:].bitcast(FP8X4), scales=scales[key][:], in_=staged[key])
+
+        mt = {}
+
+        def mask_times_t(half):
+            mt[half] = tile([P, HALF, PACK], F32, "mt%d" % half)
+            nc.vector.tensor_tensor(
+                out=mt[half][:].rearrange("p (c i) r -> p c r i", i=2),
+                in0=m_raw[half][:].rearrange("p r (c i) -> p c r i", i=2),
+                in1=t_sb[:].unsqueeze(1).unsqueeze(3).to_broadcast([P, HALF // 2, PACK, 2]),
+                op=ALU.mult,
+            )
+
+        banks = {}
+
+        def scores(pair, c):
+            for g in range(2):
+                banks[pair, c, g] = ps.tile([P, PACK, CHUNK], F32, name="score%d" % g, tag="score%d" % g, bufs=3)
+            q_key = ("q", pair, c // 2)
+            q_cols = slice(CHUNK * (c % 2), CHUNK * (c % 2 + 1))
+            for g in range(2):
+                for r in range(PACK):
+                    rows = slice(ROWS * g, ROWS * (g + 1))
+                    k_key = ("k", pair, r // 2)
+                    k_cols = slice(CHUNK * (r % 2), CHUNK * (r % 2 + 1))
+                    nc.tensor.matmul_mx(
+                        out=banks[pair, c, g][:, r, :],
+                        lhsT=codes[k_key][rows, k_cols].bitcast(FP8X4),
+                        lhsT_scale=scales[k_key][rows, k_cols],
+                        rhs=codes[q_key][rows, q_cols].bitcast(FP8X4),
+                        rhs_scale=scales[q_key][rows, q_cols],
+                        start=True,
+                        stop=True,
+                    )
+
+        p_sb = {}
+
+        def silu(pair, c):
+            p_sb[pair, c] = tile([P, 2, CHUNK, PACK], F32, "p%d_%d" % (pair, c))
+            for g in range(2):
+                nc.scalar.activation(out=p_sb[pair, c][:, g], in_=banks[pair, c, g][:].rearrange("p r q -> p q r"), func=ACT.Silu)
+
+        def weigh(pair, c):
+            w = tile([P, 2, CHUNK * PACK], BF16, "w%d_%d" % (pair, c))
+            factor = mt[c // 2][:, CHUNK * (c % 2) : CHUNK * (c % 2 + 1), :].rearrange("p q r -> p (q r)")
+            nc.vector.tensor_tensor(
+                out=w[:],
+                in0=p_sb[pair, c][:].rearrange("p g q r -> p g (q r)"),
+                in1=factor.unsqueeze(1).to_broadcast([P, 2, CHUNK * PACK]),
+                op=ALU.mult,
+            )
+            staged["w", pair, c] = w[:].rearrange("p g x -> p (g x)")
+
+        def product(y, place, pair, c, g):
+            cols = slice(CHUNK * g, CHUNK * (g + 1))
+            nc.tensor.matmul_mx(
+                out=y[:, place, :],
+                lhsT=codes["w", pair, c][:, cols].bitcast(FP8X4),
+                lhsT_scale=scales["w", pair, c][:, cols],
+                rhs=codes["v", pair, 0][:, cols].bitcast(FP8X4),
+                rhs_scale=scales["v", pair, 0][:, cols],
+                start=True,
+                stop=True,
+            )
+
+        def finish_head(pair, g):
+            y = ps.tile([P, 4, E], F32, name="y", tag="y", bufs=2)
+            for c in range(4):
+                product(y, c, pair, c, g)
+            res = tile([P, 4, E], F32, "res_head%d" % g)
+            nc.scalar.mul(out=res[:], in_=y[:], mul=1.0 / 16.0)
+            nc.sync.dma_start(out=out[2 * pair + g].rearrange("(c q) e -> q c e", q=CHUNK), in_=res[:])
+
+        def finish_chunk(pair, c):
+            y = ps.tile([P, 4, E], F32, name="y", tag="y", bufs=2)
+            for g in range(2):
+                product(y, g, pair, c, g)
+            res = tile([P, 2, E], F32, "res_chunk%d" % c)
+            nc.scalar.mul(out=res[:], in_=y[:, 0:2, :], mul=1.0 / 16.0)
+            dst = out[2 * pair : 2 * pair + 2, CHUNK * c : CHUNK * (c + 1), :].rearrange("g q e -> q g e")
+            nc.sync.dma_start(out=dst, in_=res[:])
+
+        round_k("s", 0, 1)
+        round_k("v", 0, 0)
+        quantise("k", 0, 0)
+        round_q("v", 0, 0)
+        quantise("k", 0, 1)
+        quantise("q", 0, 0)
+        scores(0, 0)
+        scores(0, 1)
+        mask_times_t(0)
+        round_q("v", 0, 1)
+        quantise("q", 0, 1)
+        silu(0, 0)
+        scores(0, 2)
+        silu(0, 1)
+        scores(0, 3)
+        silu(0, 2)
+        weigh(0, 0)
+        mask_times_t(1)
+        quantise("w", 0, 0)
+        weigh(0, 1)
+        round_k("s", 1, 0)
+        round_k("s", 1, 1)
+        silu(0, 3)
+        quantise("k", 1, 0)
+        weigh(0, 2)
+        quantise("w", 0, 1)
+        round_q("v", 1, 0)
+        quantise("k", 1, 1)
+        quantise("q", 1, 0)
+        scores(1, 0)
+        scores(1, 1)
+        round_q("s", 1, 1)
+        round_v("s", 0)
+        quantise("w", 0, 2)
+        weigh(0, 3)
+        quantise("q", 1, 1)
+        scores(1, 2)
+        quantise("v", 0, 0)
+        quantise("w", 0, 3)
+        silu(1, 0)
+        scores(1, 3)
+        silu(1, 1)
+        weigh(1, 0)
+        round_v("v", 1)
+        finish_head(0, 0)
+        finish_head(0, 1)
+        quantise("w", 1, 0)
+        weigh(1, 1)
+        quantise("v", 1, 0)
+        silu(1, 2)
+        silu(1, 3)
+        quantise("w", 1, 1)
+        weigh(1, 2)
+        finish_chunk(1, 0)
+        finish_chunk(1, 1)
+        quantise("w", 1, 2)
+        weigh(1, 3)
+        finish_chunk(1, 2)
+        quantise("w", 1, 3)
+        finish_chunk(1, 3)

@@ -42,29 +42,34 @@ def tile_rows_a_silu_mask_kernel(tc, qT, kT, t, v, mask, out):
             k_raw[pair] = tile([P, PACK, N], F32, "k_raw%d" % pair)
             nc.sync.dma_start(out=k_raw[pair][:], in_=kT[2 * pair : 2 * pair + 2].rearrange("g (p j) n -> (g p) j n", j=PACK))
 
-        def load_q(pair, first, count):
-            raw = tile([P, PACK, count * HALF], F32, "q_raw%d_%d" % (pair, first))
+        def load_q(pair, c0, count):
+            raw = tile([P, PACK, count * CHUNK], F32, "q_raw%d_%d" % (pair, c0))
             src = qT[2 * pair : 2 * pair + 2].rearrange("g (p j) n -> (g p) j n", j=PACK)
-            nc.sync.dma_start(out=raw[:], in_=src[:, :, first * HALF : (first + count) * HALF])
+            nc.sync.dma_start(out=raw[:], in_=src[:, :, c0 * CHUNK : (c0 + count) * CHUNK])
             for i in range(count):
-                q_raw[pair, first + i] = raw[:, :, i * HALF : (i + 1) * HALF]
+                q_raw[pair, c0 + i] = (raw, i)
 
-        def load_mask(half):
-            m_raw[half] = tile([P, PACK, HALF], F32, "m_raw%d" % half)
+        def load_mask(c0, count):
+            raw = tile([P, PACK, count * CHUNK], F32, "m_raw%d" % c0)
             src = mask.rearrange("(p r) q -> p r q", r=PACK)
-            nc.sync.dma_start(out=m_raw[half][:], in_=src[:, :, half * HALF : (half + 1) * HALF])
+            nc.sync.dma_start(out=raw[:], in_=src[:, :, c0 * CHUNK : (c0 + count) * CHUNK])
+            for i in range(count):
+                m_raw[c0 + i] = (raw, i)
 
         t_sb = tile([P, PACK], F32, "t_sb")
         v_raw = tile([P, H, PACK, E], F32, "v_raw")
-        load_k(0)
         nc.scalar.dma_start(out=t_sb[:], in_=t.rearrange("(p r) o -> p (r o)", r=PACK))
-        load_q(0, 0, 1)
-        load_mask(0)
-        load_q(0, 1, 1)
-        load_mask(1)
+        load_k(0)
+        load_q(0, 0, 4)
+        load_mask(0, 2)
+        load_mask(2, 2)
         load_k(1)
-        load_q(1, 0, 2)
+        load_q(1, 0, 4)
         nc.sync.dma_start(out=v_raw[:], in_=v.rearrange("h (p j) e -> p h j e", j=PACK))
+
+        warm = tile([P, 1], F32, "warm")
+        nc.vector.memset(warm[:], 0.0)
+        nc.scalar.activation(out=warm[:], in_=warm[:], func=ACT.Silu)
 
         staged, codes, scales = {}, {}, {}
 
@@ -74,11 +79,16 @@ def tile_rows_a_silu_mask_kernel(tc, qT, kT, t, v, mask, out):
             copy(engine, dst[:].rearrange("p r s j -> p s j r"), src)
             staged["k", pair, half] = dst[:].rearrange("p r s j -> p (r s j)")
 
-        def round_q(engine, pair, half):
-            dst = tile([P, HALF, PACK], BF16, "q_bf%d_%d" % (pair, half))
-            src = q_raw[pair, half].rearrange("p j (c i) -> p c j i", i=4)
+        q_place = {}
+
+        def round_q(engine, pair, c0, count):
+            dst = tile([P, count * CHUNK, PACK], BF16, "q_bf%d_%d" % (pair, c0))
+            raw, first = q_raw[pair, c0]
+            src = raw[:, :, first * CHUNK : (first + count) * CHUNK].rearrange("p j (c i) -> p c j i", i=4)
             copy(engine, dst[:].rearrange("p (c i) j -> p c j i", i=4), src)
-            staged["q", pair, half] = dst[:].rearrange("p q j -> p (q j)")
+            staged["q", pair, c0] = dst[:].rearrange("p q j -> p (q j)")
+            for i in range(count):
+                q_place[pair, c0 + i] = (("q", pair, c0), slice(CHUNK * i, CHUNK * (i + 1)))
 
         def round_v(engine, pair):
             dst = tile([P, 2, E, PACK], BF16, "v_bf%d" % pair)
@@ -88,30 +98,37 @@ def tile_rows_a_silu_mask_kernel(tc, qT, kT, t, v, mask, out):
 
         def quantise(*key):
             name = "%s%d_%d" % key
-            codes[key] = tile([P, 256], U32, "codes_" + name)
-            scales[key] = tile([P, 256], U8, "scales_" + name)
+            words = staged[key].shape[1] // PACK
+            codes[key] = tile([P, words], U32, "codes_" + name)
+            scales[key] = tile([P, words], U8, "scales_" + name)
             nc.vector.quantize_mx(out=codes[key][:].bitcast(FP8X4), scales=scales[key][:], in_=staged[key])
 
         mt = {}
 
-        def mask_times_t(half):
-            mt[half] = tile([P, HALF, PACK], F32, "mt%d" % half)
+        def mask_times_t(c0, count):
+            raw, first = m_raw[c0]
+            dst = tile([P, count * CHUNK, PACK], F32, "mt%d" % c0)
             nc.vector.tensor_tensor(
-                out=mt[half][:].rearrange("p (c i) r -> p c r i", i=2),
-                in0=m_raw[half][:].rearrange("p r (c i) -> p c r i", i=2),
-                in1=t_sb[:].unsqueeze(1).unsqueeze(3).to_broadcast([P, HALF // 2, PACK, 2]),
+                out=dst[:].rearrange("p (c i) r -> p c r i", i=2),
+                in0=raw[:, :, first * CHUNK : (first + count) * CHUNK].rearrange("p r (c i) -> p c r i", i=2),
+                in1=t_sb[:].unsqueeze(1).unsqueeze(3).to_broadcast([P, count * CHUNK // 2, PACK, 2]),
                 op=ALU.mult,
             )
+            for i in range(count):
+                mt[c0 + i] = dst[:, CHUNK * i : CHUNK * (i + 1), :]
 
         banks = {}
 
         def scores(pair, c):
             for g in range(2):
-                banks[pair, c, g] = ps.tile([P, PACK, CHUNK], F32, name="score%d" % g, tag="score%d" % g, bufs=3)
-            q_key = ("q", pair, c // 2)
-            q_cols = slice(CHUNK * (c % 2), CHUNK * (c % 2 + 1))
-            for g in range(2):
-                for r in range(PACK):
+                banks[pair, c, g] = ps.tile([P, PACK, CHUNK], F32, name="score%d" % g, tag="score%d" % g, bufs=2)
+            q_key, q_cols = q_place[pair, c]
+            if c == 0:
+                calls = [(g, r) for g in range(2) for r in range(PACK)]
+            else:
+                calls = [(g, r) for r in range(PACK) for g in range(2)]
+            for g, r in calls:
+                if True:
                     rows = slice(ROWS * g, ROWS * (g + 1))
                     k_key = ("k", pair, r // 2)
                     k_cols = slice(CHUNK * (r % 2), CHUNK * (r % 2 + 1))
@@ -132,103 +149,121 @@ def tile_rows_a_silu_mask_kernel(tc, qT, kT, t, v, mask, out):
             for g in range(2):
                 nc.scalar.activation(out=p_sb[pair, c][:, g], in_=banks[pair, c, g][:].rearrange("p r q -> p q r"), func=ACT.Silu)
 
-        def weigh(pair, c):
-            w = tile([P, 2, CHUNK * PACK], BF16, "w%d_%d" % (pair, c))
-            factor = mt[c // 2][:, CHUNK * (c % 2) : CHUNK * (c % 2 + 1), :].rearrange("p q r -> p (q r)")
+        w_place = {}
+
+        def weigh(pair, c, g0=0, count=2):
+            key = ("w", pair, 2 * c + g0)
+            w = tile([P, count, CHUNK * PACK], BF16, "w%d_%d" % key[1:])
+            factor = mt[c].rearrange("p q r -> p (q r)")
             nc.vector.tensor_tensor(
                 out=w[:],
-                in0=p_sb[pair, c][:].rearrange("p g q r -> p g (q r)"),
-                in1=factor.unsqueeze(1).to_broadcast([P, 2, CHUNK * PACK]),
+                in0=p_sb[pair, c][:, g0 : g0 + count].rearrange("p g q r -> p g (q r)"),
+                in1=factor.unsqueeze(1).to_broadcast([P, count, CHUNK * PACK]),
                 op=ALU.mult,
             )
-            staged["w", pair, c] = w[:].rearrange("p g x -> p (g x)")
+            staged[key] = w[:].rearrange("p g x -> p (g x)")
+            for i in range(count):
+                w_place[pair, c, g0 + i] = (key, slice(CHUNK * i, CHUNK * (i + 1)))
 
         def product(y, place, pair, c, g):
-            cols = slice(CHUNK * g, CHUNK * (g + 1))
+            w_key, w_cols = w_place[pair, c, g]
+            v_cols = slice(E * g, E * (g + 1))
             nc.tensor.matmul_mx(
                 out=y[:, place, :],
-                lhsT=codes["w", pair, c][:, cols].bitcast(FP8X4),
-                lhsT_scale=scales["w", pair, c][:, cols],
-                rhs=codes["v", pair, 0][:, cols].bitcast(FP8X4),
-                rhs_scale=scales["v", pair, 0][:, cols],
+                lhsT=codes[w_key][:, w_cols].bitcast(FP8X4),
+                lhsT_scale=scales[w_key][:, w_cols],
+                rhs=codes["v", pair, 0][:, v_cols].bitcast(FP8X4),
+                rhs_scale=scales["v", pair, 0][:, v_cols],
                 start=True,
                 stop=True,
             )
 
-        def finish_head(pair, g):
-            y = ps.tile([P, 4, E], F32, name="y", tag="y", bufs=2)
-            for c in range(4):
-                product(y, c, pair, c, g)
-            res = tile([P, 4, E], F32, "res_head%d" % g)
-            nc.scalar.mul(out=res[:], in_=y[:], mul=1.0 / 16.0)
-            nc.sync.dma_start(out=out[2 * pair + g].rearrange("(c q) e -> q c e", q=CHUNK), in_=res[:])
+        def scale_out(engine, dst, src):
+            if engine == "v":
+                nc.vector.tensor_scalar_mul(out=dst, in0=src, scalar1=1.0 / 16.0)
+            else:
+                nc.scalar.mul(out=dst, in_=src, mul=1.0 / 16.0)
 
-        def finish_chunk(pair, c):
-            y = ps.tile([P, 4, E], F32, name="y", tag="y", bufs=2)
+        def finish(engine, pair, g, c0, count):
+            y = ps.tile([P, 4, E], F32, name="y", tag="y", bufs=4)
+            for i in range(count):
+                product(y, i, pair, c0 + i, g)
+            res = tile([P, count, E], F32, "res%d_%d_%d" % (pair, g, c0))
+            scale_out(engine, res[:], y[:, 0:count, :])
+            dst = out[2 * pair + g, CHUNK * c0 : CHUNK * (c0 + count), :].rearrange("(c q) e -> q c e", q=CHUNK)
+            nc.sync.dma_start(out=dst, in_=res[:])
+
+        def finish_chunk(engine, pair, c):
+            y = ps.tile([P, 4, E], F32, name="y", tag="y", bufs=4)
             for g in range(2):
                 product(y, g, pair, c, g)
             res = tile([P, 2, E], F32, "res_chunk%d" % c)
-            nc.scalar.mul(out=res[:], in_=y[:, 0:2, :], mul=1.0 / 16.0)
+            scale_out(engine, res[:], y[:, 0:2, :])
             dst = out[2 * pair : 2 * pair + 2, CHUNK * c : CHUNK * (c + 1), :].rearrange("g q e -> q g e")
             nc.sync.dma_start(out=dst, in_=res[:])
 
         round_k("s", 0, 1)
         round_k("v", 0, 0)
         quantise("k", 0, 0)
-        round_q("v", 0, 0)
+        round_q("v", 0, 0, 1)
         quantise("k", 0, 1)
+        round_q("s", 0, 1, 1)
+        round_q("s", 0, 2, 2)
         quantise("q", 0, 0)
         scores(0, 0)
-        scores(0, 1)
-        mask_times_t(0)
-        round_q("v", 0, 1)
         quantise("q", 0, 1)
+        scores(0, 1)
+        mask_times_t(0, 2)
+        quantise("q", 0, 2)
+        mask_times_t(2, 2)
         silu(0, 0)
         scores(0, 2)
         silu(0, 1)
         scores(0, 3)
         silu(0, 2)
-        weigh(0, 0)
-        mask_times_t(1)
-        quantise("w", 0, 0)
-        weigh(0, 1)
         round_k("s", 1, 0)
         round_k("s", 1, 1)
+        round_q("s", 1, 0, 2)
         silu(0, 3)
-        quantise("k", 1, 0)
+        round_v("s", 0)
+        weigh(0, 0)
+        weigh(0, 1)
+        quantise("w", 0, 0)
         weigh(0, 2)
-        quantise("w", 0, 1)
-        round_q("v", 1, 0)
+        quantise("w", 0, 2)
+        quantise("k", 1, 0)
+        round_q("v", 1, 2, 2)
         quantise("k", 1, 1)
         quantise("q", 1, 0)
         scores(1, 0)
         scores(1, 1)
-        round_q("s", 1, 1)
-        round_v("s", 0)
-        quantise("w", 0, 2)
+        quantise("q", 1, 2)
+        quantise("w", 0, 4)
         weigh(0, 3)
-        quantise("q", 1, 1)
-        scores(1, 2)
-        quantise("v", 0, 0)
-        quantise("w", 0, 3)
-        silu(1, 0)
-        scores(1, 3)
-        silu(1, 1)
-        weigh(1, 0)
         round_v("v", 1)
-        finish_head(0, 0)
-        finish_head(0, 1)
-        quantise("w", 1, 0)
-        weigh(1, 1)
+        quantise("w", 0, 6)
+        quantise("v", 0, 0)
         quantise("v", 1, 0)
+        silu(1, 0)
+        scores(1, 2)
+        silu(1, 1)
+        scores(1, 3)
         silu(1, 2)
         silu(1, 3)
-        quantise("w", 1, 1)
+        finish("s", 0, 0, 0, 4)
+        finish("s", 0, 1, 0, 4)
+        weigh(1, 0)
+        weigh(1, 1)
+        quantise("w", 1, 0)
         weigh(1, 2)
-        finish_chunk(1, 0)
-        finish_chunk(1, 1)
         quantise("w", 1, 2)
-        weigh(1, 3)
-        finish_chunk(1, 2)
-        quantise("w", 1, 3)
-        finish_chunk(1, 3)
+        finish("s", 1, 0, 0, 2)
+        finish("s", 1, 1, 0, 2)
+        weigh(1, 3, 0, 1)
+        quantise("w", 1, 4)
+        finish_chunk("s", 1, 2)
+        weigh(1, 3, 1, 1)
+        quantise("w", 1, 6)
+        finish("s", 1, 0, 3, 1)
+        quantise("w", 1, 7)
+        finish("v", 1, 1, 3, 1)

@@ -73,11 +73,11 @@ def tile_rows_a_silu_mask_kernel(tc, qT, kT, t, v, mask, out):
 
         staged, codes, scales = {}, {}, {}
 
-        def round_k(engine, pair, half):
-            dst = tile([P, 2, CHUNK, PACK], BF16, "k_bf%d_%d" % (pair, half))
-            src = k_raw[pair][:].rearrange("p j (s r) -> p s j r", r=PACK)[:, :, :, 2 * half : 2 * half + 2]
+        def round_k(engine, pair):
+            dst = tile([P, PACK, CHUNK, PACK], BF16, "k_bf%d" % pair)
+            src = k_raw[pair][:].rearrange("p j (s r) -> p s j r", r=PACK)
             copy(engine, dst[:].rearrange("p r s j -> p s j r"), src)
-            staged["k", pair, half] = dst[:].rearrange("p r s j -> p (r s j)")
+            staged["k", pair, 0] = dst[:].rearrange("p r s j -> p (r s j)")
 
         q_place = {}
 
@@ -109,9 +109,9 @@ def tile_rows_a_silu_mask_kernel(tc, qT, kT, t, v, mask, out):
             raw, first = m_raw[c0]
             dst = tile([P, count * CHUNK, PACK], F32, "mt%d" % c0)
             nc.vector.tensor_tensor(
-                out=dst[:].rearrange("p (c i) r -> p c r i", i=2),
-                in0=raw[:, :, first * CHUNK : (first + count) * CHUNK].rearrange("p r (c i) -> p c r i", i=2),
-                in1=t_sb[:].unsqueeze(1).unsqueeze(3).to_broadcast([P, count * CHUNK // 2, PACK, 2]),
+                out=dst[:].rearrange("p (c i) r -> p c r i", i=4),
+                in0=raw[:, :, first * CHUNK : (first + count) * CHUNK].rearrange("p r (c i) -> p c r i", i=4),
+                in1=t_sb[:].unsqueeze(1).unsqueeze(3).to_broadcast([P, count * CHUNK // 4, PACK, 4]),
                 op=ALU.mult,
             )
             for i in range(count):
@@ -130,8 +130,8 @@ def tile_rows_a_silu_mask_kernel(tc, qT, kT, t, v, mask, out):
             for g, r in calls:
                 if True:
                     rows = slice(ROWS * g, ROWS * (g + 1))
-                    k_key = ("k", pair, r // 2)
-                    k_cols = slice(CHUNK * (r % 2), CHUNK * (r % 2 + 1))
+                    k_key = ("k", pair, 0)
+                    k_cols = slice(CHUNK * r, CHUNK * (r + 1))
                     nc.tensor.matmul_mx(
                         out=banks[pair, c, g][:, r, :],
                         lhsT=codes[k_key][rows, k_cols].bitcast(FP8X4),
@@ -202,12 +202,10 @@ def tile_rows_a_silu_mask_kernel(tc, qT, kT, t, v, mask, out):
             dst = out[2 * pair : 2 * pair + 2, CHUNK * c : CHUNK * (c + 1), :].rearrange("g q e -> q g e")
             nc.sync.dma_start(out=dst, in_=res[:])
 
-        round_k("s", 0, 1)
-        round_k("v", 0, 0)
+        round_k("v", 0)
         quantise("k", 0, 0)
         round_q("v", 0, 0, 1)
-        quantise("k", 0, 1)
-        round_q("s", 0, 1, 1)
+        round_q("v", 0, 1, 1)
         round_q("s", 0, 2, 2)
         quantise("q", 0, 0)
         scores(0, 0)
@@ -221,8 +219,7 @@ def tile_rows_a_silu_mask_kernel(tc, qT, kT, t, v, mask, out):
         silu(0, 1)
         scores(0, 3)
         silu(0, 2)
-        round_k("s", 1, 0)
-        round_k("s", 1, 1)
+        round_k("s", 1)
         round_q("s", 1, 0, 2)
         silu(0, 3)
         round_v("s", 0)
@@ -231,9 +228,8 @@ def tile_rows_a_silu_mask_kernel(tc, qT, kT, t, v, mask, out):
         quantise("w", 0, 0)
         weigh(0, 2)
         quantise("w", 0, 2)
-        quantise("k", 1, 0)
         round_q("v", 1, 2, 2)
-        quantise("k", 1, 1)
+        quantise("k", 1, 0)
         quantise("q", 1, 0)
         scores(1, 0)
         scores(1, 1)

from contextlib import ExitStack

import concourse.mybir as mybir

H, D, NQ, N, E = 4, 256, 512, 512, 128
FLOPS = 2 * H * D * N * NQ + 2 * H * N * NQ * E

F32 = mybir.dt.float32
BF16 = mybir.dt.bfloat16
U32 = mybir.dt.uint32
U8 = mybir.dt.uint8
FP8X4 = mybir.dt.float8_e4m3fn_x4
ACT = mybir.ActivationFunctionType
ALU = mybir.AluOpType

P = 128
PACK = 4
ROWS = 64
CHUNK = 128
HALF = 256


def tile_rows_a_silu_mask_kernel(tc, qT, kT, t, v, mask, out):
    nc = tc.nc
    with ExitStack() as ctx:
        sb = ctx.enter_context(tc.tile_pool(name="sb", bufs=1))
        ps = ctx.enter_context(tc.psum_pool(name="ps", bufs=1))
        ctx.enter_context(tc.manual_schedule())

        def tile(shape, dtype, name):
            return sb.tile(shape, dtype, name=name, align_bytes=64)

        def copy(engine, dst, src):
            if engine == "v":
                nc.vector.tensor_copy(out=dst, in_=src)
            else:
                nc.scalar.copy(out=dst, in_=src)

        k_raw, q_raw, m_raw = {}, {}, {}

        def load_k(pair):
            k_raw[pair] = tile([P, PACK, N], F32, "k_raw%d" % pair)
            nc.sync.dma_start(out=k_raw[pair][:], in_=kT[2 * pair : 2 * pair + 2].rearrange("g (p j) n -> (g p) j n", j=PACK))

        def load_q(pair, c0, count):
            raw = tile([P, PACK, count * CHUNK], F32, "q_raw%d_%d" % (pair, c0))
            src = qT[2 * pair : 2 * pair + 2].rearrange("g (p j) n -> (g p) j n", j=PACK)
            nc.sync.dma_start(out=raw[:], in_=src[:, :, c0 * CHUNK : (c0 + count) * CHUNK])
            for i in range(count):
                q_raw[pair, c0 + i] = (raw, i)

        def load_mask(c0, count):
            raw = tile([P, PACK, count * CHUNK], F32, "m_raw%d" % c0)
            src = mask.rearrange("(p r) q -> p r q", r=PACK)
            nc.sync.dma_start(out=raw[:], in_=src[:, :, c0 * CHUNK : (c0 + count) * CHUNK])
            for i in range(count):
                m_raw[c0 + i] = (raw, i)

        t_sb = tile([P, PACK], F32, "t_sb")
        v_raw = tile([P, H, PACK, E], F32, "v_raw")
        nc.scalar.dma_start(out=t_sb[:], in_=t.rearrange("(p r) o -> p (r o)", r=PACK))
        load_k(0)
        load_q(0, 0, 4)
        load_mask(0, 2)
        load_mask(2, 2)
        load_k(1)
        load_q(1, 0, 4)
        nc.sync.dma_start(out=v_raw[:], in_=v.rearrange("h (p j) e -> p h j e", j=PACK))

        warm = tile([P, 1], F32, "warm")
        nc.vector.memset(warm[:], 0.0)
        nc.scalar.activation(out=warm[:], in_=warm[:], func=ACT.Silu)

        staged, codes, scales = {}, {}, {}

        def round_k(engine, pair):
            dst = tile([P, PACK, CHUNK, PACK], BF16, "k_bf%d" % pair)
            src = k_raw[pair][:].rearrange("p j (s r) -> p s j r", r=PACK)
            copy(engine, dst[:].rearrange("p r s j -> p s j r"), src)
            staged["k", pair, 0] = dst[:].rearrange("p r s j -> p (r s j)")

        q_place = {}

        def round_q(engine, pair, c0, count):
            dst = tile([P, count * CHUNK, PACK], BF16, "q_bf%d_%d" % (pair, c0))
            raw, first = q_raw[pair, c0]
            src = raw[:, :, first * CHUNK : (first + count) * CHUNK].rearrange("p j (c i) -> p c j i", i=4)
            copy(engine, dst[:].rearrange("p (c i) j -> p c j i", i=4), src)
            staged["q", pair, c0] = dst[:].rearrange("p q j -> p (q j)")
            for i in range(count):
                q_place[pair, c0 + i] = (("q", pair, c0), slice(CHUNK * i, CHUNK * (i + 1)))

        def round_v(engine, pair):
            dst = tile([P, 2, E, PACK], BF16, "v_bf%d" % pair)
            src = v_raw[:, 2 * pair : 2 * pair + 2].rearrange("p g j (c i) -> p g c j i", i=4)
            copy(engine, dst[:].rearrange("p g (c i) j -> p g c j i", i=4), src)
            staged["v", pair, 0] = dst[:].rearrange("p g e j -> p (g e j)")

        def quantise(*key):
            name = "%s%d_%d" % key
            words = staged[key].shape[1] // PACK
            codes[key] = tile([P, words], U32, "codes_" + name)
            scales[key] = tile([P, words], U8, "scales_" + name)
            nc.vector.quantize_mx(out=codes[key][:].bitcast(FP8X4), scales=scales[key][:], in_=staged[key])

        mt = {}

        def mask_times_t(c0, count):
            raw, first = m_raw[c0]
            dst = tile([P, count * CHUNK, PACK], F32, "mt%d" % c0)
            nc.vector.tensor_tensor(
                out=dst[:].rearrange("p (c i) r -> p c r i", i=4),
                in0=raw[:, :, first * CHUNK : (first + count) * CHUNK].rearrange("p r (c i) -> p c r i", i=4),
                in1=t_sb[:].unsqueeze(1).unsqueeze(3).to_broadcast([P, count * CHUNK // 4, PACK, 4]),
                op=ALU.mult,
            )
            for i in range(count):
                mt[c0 + i] = dst[:, CHUNK * i : CHUNK * (i + 1), :]

        banks = {}

        def scores(pair, c):
            for g in range(2):
                banks[pair, c, g] = ps.tile([P, PACK, CHUNK], F32, name="score%d" % g, tag="score%d" % g, bufs=2)
            q_key, q_cols = q_place[pair, c]
            if c == 0:
                calls = [(g, r) for g in range(2) for r in range(PACK)]
            else:
                calls = [(g, r) for r in range(PACK) for g in range(2)]
            for g, r in calls:
                if True:
                    rows = slice(ROWS * g, ROWS * (g + 1))
                    k_key = ("k", pair, 0)
                    k_cols = slice(CHUNK * r, CHUNK * (r + 1))
                    nc.tensor.matmul_mx(
                        out=banks[pair, c, g][:, r, :],
                        lhsT=codes[k_key][rows, k_cols].bitcast(FP8X4),
                        lhsT_scale=scales[k_key][rows, k_cols],
                        rhs=codes[q_key][rows, q_cols].bitcast(FP8X4),
                        rhs_scale=scales[q_key][rows, q_cols],
                        start=True,
                        stop=True,
                    )

        p_sb = {}

        def silu(pair, c):
            p_sb[pair, c] = tile([P, 2, CHUNK, PACK], F32, "p%d_%d" % (pair, c))
            for g in range(2):
                nc.scalar.activation(out=p_sb[pair, c][:, g], in_=banks[pair, c, g][:].rearrange("p r q -> p q r"), func=ACT.Silu)

        w_place = {}

        def weigh(pair, c, g0=0, count=2):
            key = ("w", pair, 2 * c + g0)
            w = tile([P, count, CHUNK * PACK], BF16, "w%d_%d" % key[1:])
            factor = mt[c].rearrange("p q r -> p (q r)")
            nc.vector.tensor_tensor(
                out=w[:],
                in0=p_sb[pair, c][:, g0 : g0 + count].rearrange("p g q r -> p g (q r)"),
                in1=factor.unsqueeze(1).to_broadcast([P, count, CHUNK * PACK]),
                op=ALU.mult,
            )
            staged[key] = w[:].rearrange("p g x -> p (g x)")
            for i in range(count):
                w_place[pair, c, g0 + i] = (key, slice(CHUNK * i, CHUNK * (i + 1)))

        def product(y, place, pair, c, g):
            w_key, w_cols = w_place[pair, c, g]
            v_cols = slice(E * g, E * (g + 1))
            nc.tensor.matmul_mx(
                out=y[:, place, :],
                lhsT=codes[w_key][:, w_cols].bitcast(FP8X4),
                lhsT_scale=scales[w_key][:, w_cols],
                rhs=codes["v", pair, 0][:, v_cols].bitcast(FP8X4),
                rhs_scale=scales["v", pair, 0][:, v_cols],
                start=True,
                stop=True,
            )

        def scale_out(engine, dst, src):
            if engine == "v":
                nc.vector.tensor_scalar_mul(out=dst, in0=src, scalar1=1.0 / 16.0)
            else:
                nc.scalar.mul(out=dst, in_=src, mul=1.0 / 16.0)

        def finish(engine, pair, g, c0, count):
            y = ps.tile([P, 4, E], F32, name="y", tag="y", bufs=4)
            for i in range(count):
                product(y, i, pair, c0 + i, g)
            res = tile([P, count, E], F32, "res%d_%d_%d" % (pair, g, c0))
            scale_out(engine, res[:], y[:, 0:count, :])
            dst = out[2 * pair + g, CHUNK * c0 : CHUNK * (c0 + count), :].rearrange("(c q) e -> q c e", q=CHUNK)
            nc.sync.dma_start(out=dst, in_=res[:])

        def finish_chunk(engine, pair, c):
            y = ps.tile([P, 4, E], F32, name="y", tag="y", bufs=4)
            for g in range(2):
                product(y, g, pair, c, g)
            res = tile([P, 2, E], F32, "res_chunk%d" % c)
            scale_out(engine, res[:], y[:, 0:2, :])
            dst = out[2 * pair : 2 * pair + 2, CHUNK * c : CHUNK * (c + 1), :].rearrange("g q e -> q g e")
            nc.sync.dma_start(out=dst, in_=res[:])

        round_k("v", 0)
        quantise("k", 0, 0)
        round_q("v", 0, 0, 1)
        round_q("v", 0, 1, 1)
        round_q("s", 0, 2, 2)
        quantise("q", 0, 0)
        scores(0, 0)
        quantise("q", 0, 1)
        scores(0, 1)
        mask_times_t(0, 2)
        quantise("q", 0, 2)
        mask_times_t(2, 2)
        silu(0, 0)
        scores(0, 2)
        silu(0, 1)
        scores(0, 3)
        silu(0, 2)
        round_k("s", 1)
        round_q("s", 1, 0, 2)
        silu(0, 3)
        round_v("s", 0)
        weigh(0, 0)
        weigh(0, 1)
        quantise("w", 0, 0)
        weigh(0, 2)
        quantise("w", 0, 2)
        round_q("v", 1, 2, 2)
        quantise("k", 1, 0)
        quantise("q", 1, 0)
        scores(1, 0)
        scores(1, 1)
        quantise("q", 1, 2)
        quantise("w", 0, 4)
        weigh(0, 3)
        round_v("v", 1)
        quantise("w", 0, 6)
        quantise("v", 0, 0)
        quantise("v", 1, 0)
        silu(1, 0)
        scores(1, 2)
        silu(1, 1)
        scores(1, 3)
        silu(1, 2)
        silu(1, 3)
        finish("s", 0, 0, 0, 4)
        finish("s", 0, 1, 0, 4)
        weigh(1, 0)
        weigh(1, 1)
        quantise("w", 1, 0)
        weigh(1, 2)
        quantise("w", 1, 2)
        finish("s", 1, 0, 0, 2)
        finish("s", 1, 1, 0, 2)
        weigh(1, 3, 0, 1)
        quantise("w", 1, 4)
        finish_chunk("s", 1, 2)
        weigh(1, 3, 1, 1)
        quantise("w", 1, 6)
        finish("s", 1, 0, 3, 1)
        quantise("w", 1, 7)
        finish("v", 1, 1, 3, 1)
